import numpy as np
import ml_dtypes


def mxq(x, axis, fmt="e4m3"):
    dtype, down = {"e4m3": (ml_dtypes.float8_e4m3fn, 7), "e5m2": (ml_dtypes.float8_e5m2, 14)}[fmt]
    v = np.moveaxis(np.asarray(x, np.float32).astype(ml_dtypes.bfloat16).astype(np.float64), axis, -1)
    blocks = v.reshape(v.shape[:-1] + (-1, 32))
    amax = np.abs(blocks).max(-1, keepdims=True)
    byte = np.maximum(np.where(amax > 0, np.frexp(amax)[1] - 1 + 127, 0) - down, 1)
    scale = np.exp2(byte - 127.0)
    codes = (blocks / scale).astype(np.float32).astype(dtype).astype(np.float64)
    return np.moveaxis((codes * scale).reshape(v.shape), -1, axis)


WIDE = False


def mx_kscale(k):
    if not WIDE:
        return np.ones(k)
    levels = np.array([10, -10, 5, -5, 0])
    if k % 512:
        return np.exp2(np.random.permutation(np.resize(levels, k // 32))).repeat(32)
    a = np.empty((k // 512, 16))
    for p in range(k // 512):
        a[p, :8] = np.random.permutation(np.resize(levels, 8))
        for g in range(8):
            far = levels[np.abs(levels - a[p, g]) >= 10]
            a[p, g + 8] = far[np.random.randint(len(far))]
    return np.exp2(a.ravel()).repeat(32)


def f64(x):
    return np.asarray(x).astype(np.float64)


def striped(idx):
    return np.tile(idx.reshape(-1, 16).T, (8, 1)).astype(np.uint16)


def unstriped(offs):
    return offs[:16].T.reshape(-1).astype(np.int64)


def pack_weight(w):
    k, n = w.shape
    w = f64(np.asarray(w, np.float32).astype(ml_dtypes.bfloat16)).reshape(k // 32, 32, n)
    amax = np.abs(w).max(1)
    byte = np.clip(np.where(amax > 0, np.frexp(amax)[1] - 1 + 127 - 7, 1), 1, 254)
    scaled = (w * np.exp2(127.0 - byte)[:, None, :]).reshape(k, n).astype(np.float32)
    words = np.ascontiguousarray(scaled.reshape(k // 512, 128, 4, n).transpose(0, 1, 3, 2)).astype(ml_dtypes.float8_e4m3fn).view(np.uint8)
    return words, np.ascontiguousarray(byte.astype(np.uint8).reshape(k // 512, 16, n))


def unpack_weight(words, scales):
    g, p, n, _ = words.shape
    vals = np.ascontiguousarray(words).view(ml_dtypes.float8_e4m3fn).astype(np.float64) * np.repeat(np.exp2(scales.astype(np.float64) - 127.0), 8, axis=1)[..., None]
    return vals.transpose(0, 1, 3, 2).reshape(g * 512, n)


K, T, E, C, N = 1024, 2048, 4, 256, 128


def by_expert(wq, xq):
    return np.concatenate([wq[e].T @ xq[:, e * C:(e + 1) * C] for e in range(E)], axis=1)


def setup_inputs():
    n = np.random.standard_normal
    s = mx_kscale(K)[:, None]
    packed = [pack_weight(m) for m in n((E, K, N)) / np.sqrt(K) / s[None]]
    return {
        "xT": (n((K, T)) * s).astype(np.float32),
        "w_words": np.stack([m[0] for m in packed]),
        "w_scales": np.stack([m[1] for m in packed]),
        "gate": np.tile(np.random.uniform(0.2, 1.0, E * C), (N, 1)).astype(np.float32),
        "offs": striped(np.random.permutation(T)[:E * C]),
    }


def reference(xT, w_words, w_scales, gate, offs):
    idx = unstriped(offs)
    xq = mxq(f64(xT)[:, idx], 0, "e4m3")
    w = np.stack([unpack_weight(w_words[e], w_scales[e]) for e in range(E)])
    y = by_expert(w, xq)
    out = np.zeros((N, T))
    out[:, idx] = f64(gate) * y
    return out

@@ -1,0 +1,134 @@
+from contextlib import ExitStack
+
+import concourse.mybir as mybir
+
+K, T, E, C, N = 1024, 2048, 4, 256, 128
+FLOPS = 2 * K * N * E * C
+
+F32 = mybir.dt.float32
+BF16 = mybir.dt.bfloat16
+I32 = mybir.dt.int32
+U32 = mybir.dt.uint32
+U16 = mybir.dt.uint16
+U8 = mybir.dt.uint8
+FP8X4 = mybir.dt.float8_e4m3fn_x4
+MULT = mybir.AluOpType.mult
+ADD = mybir.AluOpType.add
+
+P = 128
+SLOTS = E * C
+PASSES = K // 512
+WINDOWS = 2 * PASSES
+
+CUTS = [[[2048,1152,0]],[[1024,576,448],[1024,576,448]],[[1024,640,384],[1024,576,448]],[[1024,480,544],[512,288,224],[256,160,0],[256,0,0]]]
+GATHER_CUTS = ((1024,),(1024,),(1024,),(1024,),)
+QUANT_CUTS = ((1024,),(256,256,512,),)
+SCATTER_CUTS = (1,3,)
+GP_PIECE = 1024
+SCALES_AFTER = 9
+
+
+def tile_routed_moe_kernel(tc, xT, w_words, w_scales, gate, offs, out):
+    nc = tc.nc
+    with ExitStack() as ctx:
+        lists = ctx.enter_context(tc.tile_pool(name="lists", bufs=1))
+        keep = ctx.enter_context(tc.tile_pool(name="keep", bufs=1))
+        psum = ctx.enter_context(tc.psum_pool(name="psum", bufs=1))
+
+        offs_t = lists.tile([P, SLOTS // 16], U16, name="offs_t")
+
+        w_scale_t = keep.tile([P, E * PASSES, N], U8, name="w_scale_t", align_bytes=64)
+        nc.vector.memset(w_scale_t[:].rearrange("p i n -> p (i n)").bitcast(I32), 0)
+        out_t = keep.tile([P, T], F32, name="out_t")
+        nc.vector.memset(out_t[:], 0.0)
+
+        planes = xT.rearrange("(g p t) n -> g p t n", p=P, t=4)
+        scale_rows = w_scales.rearrange("e a (q r) n -> r q (e a) n", r=4)
+        raws = []
+        loads = 0
+        for w in range(WINDOWS):
+            g, u = divmod(w, 2)
+            c0 = 0
+            for cols, s_cols, g_cols in CUTS[w]:
+                raw = keep.tile([P, 2, cols], F32, name="raw%d_%d" % (w, c0))
+                nc.sync.dma_start(out=raw[:], in_=planes[g, :, 2 * u : 2 * u + 2, c0 : c0 + cols])
+                raws.append((w, c0, cols, s_cols, g_cols, raw))
+                c0 += cols
+                loads += 1
+                if loads == 1:
+                    nc.sync.dma_start(offs_t[:], offs)
+                if loads == SCALES_AFTER:
+                    for r in range(4):
+                        nc.sync.dma_start(out=w_scale_t[r:P:32, :, :].bitcast(I32), in_=scale_rows[r].bitcast(I32))
+
+        w_code_t = keep.tile([P, E * PASSES, N], I32, name="w_code_t", align_bytes=64)
+        nc.sync.dma_start(out=w_code_t[:], in_=w_words.rearrange("e a p n r -> p (e a) (n r)").bitcast(I32))
+        gate_t = keep.tile([P, SLOTS], F32, name="gate_t")
+        nc.sync.dma_start(out=gate_t[:], in_=gate)
+
+        pairs = [keep.tile([P, 2 * T], BF16, name="pair%d" % w) for w in range(WINDOWS)]
+        grouped = [keep.tile([P, 4 * SLOTS], BF16, name="grouped%d" % g, align_bytes=64) for g in range(PASSES)]
+        codes = [keep.tile([P, SLOTS], U32, name="codes%d" % g, align_bytes=64) for g in range(PASSES)]
+        scales = [keep.tile([P, SLOTS], U8, name="scales%d" % g, align_bytes=64) for g in range(PASSES)]
+        acc = [psum.tile([P, C], F32, name="acc%d" % e) for e in range(E)]
+
+        for w in range(WINDOWS):
+            g, u = divmod(w, 2)
+            for ww, c0, cols, s_cols, g_cols, raw in raws:
+                if ww != w:
+                    continue
+                src = raw[:].rearrange("p e n -> p n e")
+                dst = pairs[w][:, 2 * c0 : 2 * (c0 + cols)].rearrange("p (n e) -> p n e", e=2)
+                if s_cols > 0:
+                    nc.scalar.copy(out=dst[:, 0:s_cols, :], in_=src[:, 0:s_cols, :])
+                for a in range(s_cols, s_cols + g_cols, GP_PIECE):
+                    b = min(a + GP_PIECE, s_cols + g_cols)
+                    nc.gpsimd.tensor_scalar(
+                        out=dst[:, a:b, :], in0=src[:, a:b, :], scalar1=1.0, scalar2=0.0, op0=MULT, op1=ADD
+                    )
+                if s_cols + g_cols < cols:
+                    nc.vector.tensor_copy(out=dst[:, s_cols + g_cols :, :], in_=src[:, s_cols + g_cols :, :])
+            window = pairs[w][:].bitcast(U32)
+            words = grouped[g][:].bitcast(U32).rearrange("p (j u) -> p j u", u=2)
+            j0 = 0
+            for n in GATHER_CUTS[w]:
+                nc.vector.tensor_copy(
+                    out=words[:, j0 : j0 + n, u],
+                    in_=window.indirect(offs_t[:, j0 // 16 : (j0 + n) // 16]),
+                )
+                j0 += n
+            if u == 1:
+                j0 = 0
+                for n in QUANT_CUTS[g]:
+                    nc.vector.quantize_mx(
+                        out=codes[g][:, j0 : j0 + n].bitcast(FP8X4),
+                        scales=scales[g][:, j0 : j0 + n],
+                        in_=grouped[g][:, 4 * j0 : 4 * (j0 + n)],
+                    )
+                    j0 += n
+                for e in range(E):
+                    js = slice(e * C, (e + 1) * C)
+                    nc.tensor.matmul_mx(
+                        out=acc[e][:],
+                        lhsT=w_code_t[:, PASSES * e + g, :].bitcast(FP8X4),
+                        lhsT_scale=w_scale_t[:, PASSES * e + g, :],
+                        rhs=codes[g][:, js].bitcast(FP8X4),
+                        rhs_scale=scales[g][:, js],
+                        start=(g == 0),
+                        stop=(g == PASSES - 1),
+                    )
+
+        e0 = 0
+        for s, experts in enumerate(SCATTER_CUTS):
+            y = keep.tile([P, experts * C], F32, name="y%d" % s)
+            for i in range(experts):
+                nc.scalar.copy(out=y[:, i * C : (i + 1) * C], in_=acc[e0 + i][:])
+            j0, j1 = e0 * C, (e0 + experts) * C
+            nc.vector.tensor_tensor(
+                out=out_t[:].indirect(offs_t[:, j0 // 16 : j1 // 16]),
+                in0=y[:],
+                in1=gate_t[:, j0:j1],
+                op=MULT,
+            )
+            e0 += experts
+        nc.sync.dma_start(out=out, in_=out_t[:])

@@ -20,7 +20,7 @@ SLOTS = E * C
 PASSES = K // 512
 WINDOWS = 2 * PASSES
 
-CUTS = [[[2048,1152,0]],[[1024,576,448],[1024,576,448]],[[1024,640,384],[1024,576,448]],[[1024,480,544],[512,288,224],[256,160,0],[256,0,0]]]
+CUTS = [[[1024,256,224],[1024,256,224]],[[1024,576,448],[1024,576,448]],[[1024,640,384],[1024,576,448]],[[1024,480,544],[512,288,224],[256,160,0],[256,0,0]]]
 GATHER_CUTS = ((1024,),(1024,),(1024,),(1024,),)
 QUANT_CUTS = ((1024,),(256,256,512,),)
 SCATTER_CUTS = (1,3,)

@@ -14,18 +14,23 @@ U8 = mybir.dt.uint8
 FP8X4 = mybir.dt.float8_e4m3fn_x4
 MULT = mybir.AluOpType.mult
 ADD = mybir.AluOpType.add
+COPY = mybir.ActivationFunctionType.Copy
 
 P = 128
 SLOTS = E * C
 PASSES = K // 512
-WINDOWS = 2 * PASSES
 
-CUTS = [[[1024,256,224],[1024,256,224]],[[1024,576,448],[1024,576,448]],[[1024,640,384],[1024,576,448]],[[1024,480,544],[512,288,224],[256,160,0],[256,0,0]]]
-GATHER_CUTS = ((1024,),(1024,),(1024,),(1024,),)
-QUANT_CUTS = ((1024,),(256,256,512,),)
-SCATTER_CUTS = (1,3,)
-GP_PIECE = 1024
-SCALES_AFTER = 9
+UNITS = (
+    (0, "pair", 0, ((1024, 352, 0), (1024, 352, 0))),
+    (0, "pair", 1, ((1024, 576, 448), (512, 288, 224), (512, 160, 0))),
+    (1, "plane", 0, ((1024, 0, 1024), (1024, 448, 576))),
+    (1, "plane", 1, ((1024, 0, 1024), (1024, 448, 576))),
+    (1, "plane", 2, ((1024, 0, 1024), (1024, 448, 576))),
+    (1, "plane", 3, ((1024, 0, 1024), (512, 0, 512), (512, 512, 0))),
+)
+A_SLOTS = 576
+QUANT_CUTS = ((1024,), (256, 256, 512))
+SCATTER_CUTS = (1, 3)
 
 
 def tile_routed_moe_kernel(tc, xT, w_words, w_scales, gate, offs, out):
@@ -44,60 +49,84 @@ def tile_routed_moe_kernel(tc, xT, w_words, w_scales, gate, offs, out):
 
         planes = xT.rearrange("(g p t) n -> g p t n", p=P, t=4)
         scale_rows = w_scales.rearrange("e a (q r) n -> r q (e a) n", r=4)
-        raws = []
-        loads = 0
-        for w in range(WINDOWS):
-            g, u = divmod(w, 2)
-            c0 = 0
-            for cols, s_cols, g_cols in CUTS[w]:
-                raw = keep.tile([P, 2, cols], F32, name="raw%d_%d" % (w, c0))
-                nc.sync.dma_start(out=raw[:], in_=planes[g, :, 2 * u : 2 * u + 2, c0 : c0 + cols])
-                raws.append((w, c0, cols, s_cols, g_cols, raw))
-                c0 += cols
-                loads += 1
-                if loads == 1:
-                    nc.sync.dma_start(offs_t[:], offs)
-                if loads == SCALES_AFTER:
-                    for r in range(4):
-                        nc.sync.dma_start(out=w_scale_t[r:P:32, :, :].bitcast(I32), in_=scale_rows[r].bitcast(I32))
 
+        raws = []
+        first = True
+        for g, kind, i, cuts in UNITS:
+            if kind == "pair":
+                raw = keep.tile([P, 2, T], F32, name="rawpair%d_%d" % (g, i))
+            else:
+                raw = keep.tile([P, T], F32, name="rawplane%d_%d" % (g, i))
+            raws.append(raw)
+            c0 = 0
+            for cols, s_cols, g_cols in cuts:
+                if kind == "pair":
+                    nc.sync.dma_start(out=raw[:, :, c0 : c0 + cols], in_=planes[g, :, 2 * i : 2 * i + 2, c0 : c0 + cols])
+                else:
+                    nc.sync.dma_start(out=raw[:, c0 : c0 + cols], in_=planes[g, :, i, c0 : c0 + cols])
+                c0 += cols
+                if first:
+                    nc.sync.dma_start(offs_t[:], offs)
+                    first = False
+        for r in range(4):
+            nc.sync.dma_start(out=w_scale_t[r:P:32, :, :].bitcast(I32), in_=scale_rows[r].bitcast(I32))
         w_code_t = keep.tile([P, E * PASSES, N], I32, name="w_code_t", align_bytes=64)
         nc.sync.dma_start(out=w_code_t[:], in_=w_words.rearrange("e a p n r -> p (e a) (n r)").bitcast(I32))
         gate_t = keep.tile([P, SLOTS], F32, name="gate_t")
         nc.sync.dma_start(out=gate_t[:], in_=gate)
 
-        pairs = [keep.tile([P, 2 * T], BF16, name="pair%d" % w) for w in range(WINDOWS)]
         grouped = [keep.tile([P, 4 * SLOTS], BF16, name="grouped%d" % g, align_bytes=64) for g in range(PASSES)]
         codes = [keep.tile([P, SLOTS], U32, name="codes%d" % g, align_bytes=64) for g in range(PASSES)]
         scales = [keep.tile([P, SLOTS], U8, name="scales%d" % g, align_bytes=64) for g in range(PASSES)]
         acc = [psum.tile([P, C], F32, name="acc%d" % e) for e in range(E)]
 
-        for w in range(WINDOWS):
-            g, u = divmod(w, 2)
-            for ww, c0, cols, s_cols, g_cols, raw in raws:
-                if ww != w:
-                    continue
-                src = raw[:].rearrange("p e n -> p n e")
-                dst = pairs[w][:, 2 * c0 : 2 * (c0 + cols)].rearrange("p (n e) -> p n e", e=2)
-                if s_cols > 0:
-                    nc.scalar.copy(out=dst[:, 0:s_cols, :], in_=src[:, 0:s_cols, :])
-                for a in range(s_cols, s_cols + g_cols, GP_PIECE):
-                    b = min(a + GP_PIECE, s_cols + g_cols)
-                    nc.gpsimd.tensor_scalar(
-                        out=dst[:, a:b, :], in0=src[:, a:b, :], scalar1=1.0, scalar2=0.0, op0=MULT, op1=ADD
-                    )
-                if s_cols + g_cols < cols:
-                    nc.vector.tensor_copy(out=dst[:, s_cols + g_cols :, :], in_=src[:, s_cols + g_cols :, :])
-            window = pairs[w][:].bitcast(U32)
-            words = grouped[g][:].bitcast(U32).rearrange("p (j u) -> p j u", u=2)
-            j0 = 0
-            for n in GATHER_CUTS[w]:
-                nc.vector.tensor_copy(
-                    out=words[:, j0 : j0 + n, u],
-                    in_=window.indirect(offs_t[:, j0 // 16 : (j0 + n) // 16]),
+        def cast(dst, src, cols, s_cols, g_cols):
+            if s_cols > 0:
+                nc.scalar.copy(out=dst[:, 0:s_cols], in_=src[:, 0:s_cols])
+            if g_cols > 0:
+                nc.gpsimd.tensor_scalar(
+                    out=dst[:, s_cols : s_cols + g_cols],
+                    in0=src[:, s_cols : s_cols + g_cols],
+                    scalar1=1.0,
+                    scalar2=0.0,
+                    op0=MULT,
+                    op1=ADD,
                 )
-                j0 += n
-            if u == 1:
+            if s_cols + g_cols < cols:
+                nc.vector.tensor_copy(out=dst[:, s_cols + g_cols : cols], in_=src[:, s_cols + g_cols : cols])
+
+        done = [0] * PASSES
+        for (g, kind, i, cuts), raw in zip(UNITS, raws):
+            if kind == "pair":
+                pair = keep.tile([P, 2 * T], BF16, name="pair%d_%d" % (g, i))
+                c0 = 0
+                for cols, s_cols, g_cols in cuts:
+                    cast(
+                        pair[:, 2 * c0 : 2 * (c0 + cols)].rearrange("p (n e) -> p n e", e=2),
+                        raw[:, :, c0 : c0 + cols].rearrange("p e n -> p n e"),
+                        cols,
+                        s_cols,
+                        g_cols,
+                    )
+                    c0 += cols
+                words = grouped[g][:].bitcast(U32).rearrange("p (j u) -> p j u", u=2)
+                nc.vector.tensor_copy(out=words[:, :, i], in_=pair[:].bitcast(U32).indirect(offs_t[:]))
+                done[g] += 2
+            else:
+                plane = keep.tile([P, T], BF16, name="plane%d_%d" % (g, i))
+                c0 = 0
+                for cols, s_cols, g_cols in cuts:
+                    cast(plane[:, c0 : c0 + cols], raw[:, c0 : c0 + cols], cols, s_cols, g_cols)
+                    c0 += cols
+                values = grouped[g][:].rearrange("p (j t) -> p j t", t=4)
+                nc.vector.tensor_copy(out=values[:, 0:A_SLOTS, i], in_=raw[:].indirect(offs_t[:, 0 : A_SLOTS // 16]))
+                nc.scalar.activation(
+                    out=values[:, A_SLOTS:SLOTS, i],
+                    in_=plane[:].indirect(offs_t[:, A_SLOTS // 16 : SLOTS // 16]),
+                    func=COPY,
+                )
+                done[g] += 1
+            if done[g] == 4:
                 j0 = 0
                 for n in QUANT_CUTS[g]:
                     nc.vector.quantize_mx(

@@ -23,13 +23,13 @@ PASSES = K // 512
 UNITS = (
     (0, "pair", 0, ((1024, 352, 0), (1024, 352, 0))),
     (0, "pair", 1, ((1024, 576, 448), (512, 288, 224), (512, 160, 0))),
-    (1, "plane", 0, ((1024, 0, 1024), (1024, 448, 576))),
-    (1, "plane", 1, ((1024, 0, 1024), (1024, 448, 576))),
-    (1, "plane", 2, ((1024, 0, 1024), (1024, 448, 576))),
+    (1, "pair", 0, ((1024, 480, 544), (512, 288, 224), (256, 160, 0), (256, 0, 0))),
+    (1, "plane", 2, ((1024, 448, 576), (512, 320, 192), (512, 256, 256))),
     (1, "plane", 3, ((1024, 0, 1024), (512, 0, 512), (512, 512, 0))),
 )
-A_SLOTS = 576
-QUANT_CUTS = ((1024,), (256, 256, 512))
+A_SLOTS = 512
+S_PIECES = (256, 256)
+QUANT_CUTS = ((1024,), (256, 256, 256, 256))
 SCATTER_CUTS = (1, 3)
 
 
@@ -120,11 +120,14 @@ def tile_routed_moe_kernel(tc, xT, w_words, w_scales, gate, offs, out):
                     c0 += cols
                 values = grouped[g][:].rearrange("p (j t) -> p j t", t=4)
                 nc.vector.tensor_copy(out=values[:, 0:A_SLOTS, i], in_=raw[:].indirect(offs_t[:, 0 : A_SLOTS // 16]))
-                nc.scalar.activation(
-                    out=values[:, A_SLOTS:SLOTS, i],
-                    in_=plane[:].indirect(offs_t[:, A_SLOTS // 16 : SLOTS // 16]),
-                    func=COPY,
-                )
+                j0 = A_SLOTS
+                for n in S_PIECES:
+                    nc.scalar.activation(
+                        out=values[:, j0 : j0 + n, i],
+                        in_=plane[:].indirect(offs_t[:, j0 // 16 : (j0 + n) // 16]),
+                        func=COPY,
+                    )
+                    j0 += n
                 done[g] += 1
             if done[g] == 4:
                 j0 = 0

@@ -138,17 +138,18 @@ def tile_routed_moe_kernel(tc, xT, w_words, w_scales, gate, offs, out):
                         in_=grouped[g][:, 4 * j0 : 4 * (j0 + n)],
                     )
                     j0 += n
-                for e in range(E):
-                    js = slice(e * C, (e + 1) * C)
-                    nc.tensor.matmul_mx(
-                        out=acc[e][:],
-                        lhsT=w_code_t[:, PASSES * e + g, :].bitcast(FP8X4),
-                        lhsT_scale=w_scale_t[:, PASSES * e + g, :],
-                        rhs=codes[g][:, js].bitcast(FP8X4),
-                        rhs_scale=scales[g][:, js],
-                        start=(g == 0),
-                        stop=(g == PASSES - 1),
-                    )
+
+        for g, e in ((0, 0), (1, 0), (0, 1), (0, 2), (0, 3), (1, 1), (1, 2), (1, 3)):
+            js = slice(e * C, (e + 1) * C)
+            nc.tensor.matmul_mx(
+                out=acc[e][:],
+                lhsT=w_code_t[:, PASSES * e + g, :].bitcast(FP8X4),
+                lhsT_scale=w_scale_t[:, PASSES * e + g, :],
+                rhs=codes[g][:, js].bitcast(FP8X4),
+                rhs_scale=scales[g][:, js],
+                start=(g == 0),
+                stop=(g == PASSES - 1),
+            )
 
         e0 = 0
         for s, experts in enumerate(SCATTER_CUTS):

@@ -27,8 +27,8 @@ UNITS = (
     (1, "plane", 2, ((1024, 448, 576), (512, 320, 192), (512, 256, 256))),
     (1, "plane", 3, ((1024, 0, 1024), (512, 0, 512), (512, 512, 0))),
 )
-A_SLOTS = 512
-S_PIECES = (256, 256)
+A_SLOTS = 256
+S_PIECES = (256, 256, 256)
 QUANT_CUTS = ((1024,), (256, 256, 256, 256))
 SCATTER_CUTS = (1, 3)
 

@@ -23,12 +23,12 @@ PASSES = K // 512
 UNITS = (
     (0, "pair", 0, ((1024, 352, 0), (1024, 352, 0))),
     (0, "pair", 1, ((1024, 576, 448), (512, 288, 224), (512, 160, 0))),
-    (1, "pair", 0, ((1024, 480, 544), (512, 288, 224), (256, 160, 0), (256, 0, 0))),
+    (1, "pair", 0, ((1024, 480, 544), (512, 288, 224), (256, 160, 96), (256, 128, 128))),
     (1, "plane", 2, ((1024, 448, 576), (512, 320, 192), (512, 256, 256))),
     (1, "plane", 3, ((1024, 0, 1024), (512, 0, 512), (512, 512, 0))),
 )
-A_SLOTS = 256
-S_PIECES = (256, 256, 256)
+A_SLOTS = 384
+S_PIECES = (384, 256)
 QUANT_CUTS = ((1024,), (256, 256, 256, 256))
 SCATTER_CUTS = (1, 3)
 

@@ -25,10 +25,10 @@ UNITS = (
     (0, "pair", 1, ((1024, 576, 448), (512, 288, 224), (512, 160, 0))),
     (1, "pair", 0, ((1024, 480, 544), (512, 288, 224), (256, 160, 96), (256, 128, 128))),
     (1, "plane", 2, ((1024, 448, 576), (512, 320, 192), (512, 256, 256))),
-    (1, "plane", 3, ((1024, 0, 1024), (512, 0, 512), (512, 512, 0))),
+    (1, "plane", 3, ((1024, 0, 1024), (768, 0, 768), (256, 256, 0))),
 )
-A_SLOTS = 384
-S_PIECES = (384, 256)
+A_SLOTS = 320
+S_PIECES = (448, 256)
 QUANT_CUTS = ((1024,), (256, 256, 256, 256))
 SCATTER_CUTS = (1, 3)
 

@@ -1,6 +1,7 @@
 from contextlib import ExitStack
 
 import concourse.mybir as mybir
+from concourse.masks import make_identity
 
 K, T, E, C, N = 1024, 2048, 4, 256, 128
 FLOPS = 2 * K * N * E * C
@@ -47,6 +48,16 @@ def tile_routed_moe_kernel(tc, xT, w_words, w_scales, gate, offs, out):
         out_t = keep.tile([P, T], F32, name="out_t")
         nc.vector.memset(out_t[:], 0.0)
 
+        ident = keep.tile([P, P], F32, name="ident")
+        make_identity(nc, ident[:])
+        gate_rows = keep.tile([P, P], F32, name="gate_rows")
+        nc.gpsimd.memset(gate_rows[:], 0.0)
+        nc.scalar.dma_start(out=gate_rows[0 : SLOTS // P, :], in_=gate[0, :].rearrange("(c n) -> c n", n=P))
+        cols_bank = psum.tile([P, P], F32, name="cols_bank")
+        nc.tensor.transpose(cols_bank[:], gate_rows[:], ident[:])
+        gate_cols = keep.tile([P, SLOTS // P], F32, name="gate_cols")
+        nc.scalar.copy(out=gate_cols[:], in_=cols_bank[:, 0 : SLOTS // P])
+
         planes = xT.rearrange("(g p t) n -> g p t n", p=P, t=4)
         scale_rows = w_scales.rearrange("e a (q r) n -> r q (e a) n", r=4)
 
@@ -73,7 +84,11 @@ def tile_routed_moe_kernel(tc, xT, w_words, w_scales, gate, offs, out):
         w_code_t = keep.tile([P, E * PASSES, N], I32, name="w_code_t", align_bytes=64)
         nc.sync.dma_start(out=w_code_t[:], in_=w_words.rearrange("e a p n r -> p (e a) (n r)").bitcast(I32))
         gate_t = keep.tile([P, SLOTS], F32, name="gate_t")
-        nc.sync.dma_start(out=gate_t[:], in_=gate)
+        for h in range(2):
+            bank = psum.tile([P, SLOTS // 2], F32, name="gate_bank%d" % h)
+            for c in range(4):
+                nc.tensor.transpose(bank[:, c * P : (c + 1) * P], gate_cols[:, 4 * h + c : 4 * h + c + 1].to_broadcast([P, P]), ident[:])
+            nc.scalar.copy(out=gate_t[:, h * SLOTS // 2 : (h + 1) * SLOTS // 2], in_=bank[:])
 
         grouped = [keep.tile([P, 4 * SLOTS], BF16, name="grouped%d" % g, align_bytes=64) for g in range(PASSES)]
         codes = [keep.tile([P, SLOTS], U32, name="codes%d" % g, align_bytes=64) for g in range(PASSES)]

@@ -22,14 +22,14 @@ SLOTS = E * C
 PASSES = K // 512
 
 UNITS = (
-    (0, "pair", 0, ((1024, 352, 0), (1024, 352, 0))),
-    (0, "pair", 1, ((1024, 576, 448), (512, 288, 224), (512, 160, 0))),
-    (1, "pair", 0, ((1024, 480, 544), (512, 288, 224), (256, 160, 96), (256, 128, 128))),
-    (1, "plane", 2, ((1024, 448, 576), (512, 320, 192), (512, 256, 256))),
-    (1, "plane", 3, ((1024, 0, 1024), (768, 0, 768), (256, 256, 0))),
+    (0, "plane", 0, ((2048, 0, 0),), 1024, ()),
+    (0, "plane", 1, ((2048, 0, 0),), 1024, ()),
+    (0, "plane", 2, ((1024, 512, 512), (1024, 512, 512)), 512, (512,)),
+    (0, "plane", 3, ((1024, 256, 768), (1024, 512, 512)), 512, (512,)),
+    (1, "pair", 0, ((1024, 512, 512), (1024, 384, 256)), 0, ()),
+    (1, "plane", 2, ((1024, 512, 512), (512, 256, 256), (512, 256, 256)), 320, (704,)),
+    (1, "plane", 3, ((1024, 0, 1024), (768, 0, 768), (256, 256, 0)), 320, (448, 256)),
 )
-A_SLOTS = 320
-S_PIECES = (448, 256)
 QUANT_CUTS = ((1024,), (256, 256, 256, 256))
 SCATTER_CUTS = (1, 3)
 
@@ -43,6 +43,8 @@ def tile_routed_moe_kernel(tc, xT, w_words, w_scales, gate, offs, out):
 
         offs_t = lists.tile([P, SLOTS // 16], U16, name="offs_t")
 
+        gate_rows = keep.tile([P, P], F32, name="gate_rows")
+        nc.vector.memset(gate_rows[:], 0.0)
         w_scale_t = keep.tile([P, E * PASSES, N], U8, name="w_scale_t", align_bytes=64)
         nc.vector.memset(w_scale_t[:].rearrange("p i n -> p (i n)").bitcast(I32), 0)
         out_t = keep.tile([P, T], F32, name="out_t")
@@ -50,9 +52,7 @@ def tile_routed_moe_kernel(tc, xT, w_words, w_scales, gate, offs, out):
 
         ident = keep.tile([P, P], F32, name="ident")
         make_identity(nc, ident[:])
-        gate_rows = keep.tile([P, P], F32, name="gate_rows")
-        nc.gpsimd.memset(gate_rows[:], 0.0)
-        nc.scalar.dma_start(out=gate_rows[0 : SLOTS // P, :], in_=gate[0, :].rearrange("(c n) -> c n", n=P))
+        nc.sync.dma_start(out=gate_rows[0 : SLOTS // P, :], in_=gate[0, :].rearrange("(c n) -> c n", n=P))
         cols_bank = psum.tile([P, P], F32, name="cols_bank")
         nc.tensor.transpose(cols_bank[:], gate_rows[:], ident[:])
         gate_cols = keep.tile([P, SLOTS // P], F32, name="gate_cols")
@@ -63,7 +63,7 @@ def tile_routed_moe_kernel(tc, xT, w_words, w_scales, gate, offs, out):
 
         raws = []
         first = True
-        for g, kind, i, cuts in UNITS:
+        for g, kind, i, cuts, v_slots, s_pieces in UNITS:
             if kind == "pair":
                 raw = keep.tile([P, 2, T], F32, name="rawpair%d_%d" % (g, i))
             else:
@@ -111,7 +111,7 @@ def tile_routed_moe_kernel(tc, xT, w_words, w_scales, gate, offs, out):
                 nc.vector.tensor_copy(out=dst[:, s_cols + g_cols : cols], in_=src[:, s_cols + g_cols : cols])
 
         done = [0] * PASSES
-        for (g, kind, i, cuts), raw in zip(UNITS, raws):
+        for (g, kind, i, cuts, v_slots, s_pieces), raw in zip(UNITS, raws):
             if kind == "pair":
                 pair = keep.tile([P, 2 * T], BF16, name="pair%d_%d" % (g, i))
                 c0 = 0
@@ -128,15 +128,16 @@ def tile_routed_moe_kernel(tc, xT, w_words, w_scales, gate, offs, out):
                 nc.vector.tensor_copy(out=words[:, :, i], in_=pair[:].bitcast(U32).indirect(offs_t[:]))
                 done[g] += 2
             else:
-                plane = keep.tile([P, T], BF16, name="plane%d_%d" % (g, i))
-                c0 = 0
-                for cols, s_cols, g_cols in cuts:
-                    cast(plane[:, c0 : c0 + cols], raw[:, c0 : c0 + cols], cols, s_cols, g_cols)
-                    c0 += cols
                 values = grouped[g][:].rearrange("p (j t) -> p j t", t=4)
-                nc.vector.tensor_copy(out=values[:, 0:A_SLOTS, i], in_=raw[:].indirect(offs_t[:, 0 : A_SLOTS // 16]))
-                j0 = A_SLOTS
-                for n in S_PIECES:
+                nc.vector.tensor_copy(out=values[:, 0:v_slots, i], in_=raw[:].indirect(offs_t[:, 0 : v_slots // 16]))
+                if s_pieces:
+                    plane = keep.tile([P, T], BF16, name="plane%d_%d" % (g, i))
+                    c0 = 0
+                    for cols, s_cols, g_cols in cuts:
+                        cast(plane[:, c0 : c0 + cols], raw[:, c0 : c0 + cols], cols, s_cols, g_cols)
+                        c0 += cols
+                j0 = v_slots
+                for n in s_pieces:
                     nc.scalar.activation(
                         out=values[:, j0 : j0 + n, i],
                         in_=plane[:].indirect(offs_t[:, j0 // 16 : (j0 + n) // 16]),

@@ -22,13 +22,13 @@ SLOTS = E * C
 PASSES = K // 512
 
 UNITS = (
-    (0, "plane", 0, ((2048, 0, 0),), 1024, ()),
-    (0, "plane", 1, ((2048, 0, 0),), 1024, ()),
-    (0, "plane", 2, ((1024, 512, 512), (1024, 512, 512)), 512, (512,)),
-    (0, "plane", 3, ((1024, 256, 768), (1024, 512, 512)), 512, (512,)),
-    (1, "pair", 0, ((1024, 512, 512), (1024, 384, 256)), 0, ()),
+    (0, "plane", 0, ((2048, 512, 768),), 640, (384,)),
+    (0, "plane", 1, ((2048, 512, 1536),), 640, (384,)),
+    (0, "plane", 2, ((2048, 512, 1536),), 640, (384,)),
+    (0, "plane", 3, ((2048, 512, 1536),), 640, (384,)),
+    (1, "pair", 0, ((1024, 512, 512), (1024, 256, 0)), 0, ()),
     (1, "plane", 2, ((1024, 512, 512), (512, 256, 256), (512, 256, 256)), 320, (704,)),
-    (1, "plane", 3, ((1024, 0, 1024), (768, 0, 768), (256, 256, 0)), 320, (448, 256)),
+    (1, "plane", 3, ((768, 0, 768), (768, 0, 768), (512, 256, 256)), 320, (448, 256)),
 )
 QUANT_CUTS = ((1024,), (256, 256, 256, 256))
 SCATTER_CUTS = (1, 3)
@@ -129,13 +129,13 @@ def tile_routed_moe_kernel(tc, xT, w_words, w_scales, gate, offs, out):
                 done[g] += 2
             else:
                 values = grouped[g][:].rearrange("p (j t) -> p j t", t=4)
-                nc.vector.tensor_copy(out=values[:, 0:v_slots, i], in_=raw[:].indirect(offs_t[:, 0 : v_slots // 16]))
                 if s_pieces:
                     plane = keep.tile([P, T], BF16, name="plane%d_%d" % (g, i))
                     c0 = 0
                     for cols, s_cols, g_cols in cuts:
                         cast(plane[:, c0 : c0 + cols], raw[:, c0 : c0 + cols], cols, s_cols, g_cols)
                         c0 += cols
+                nc.vector.tensor_copy(out=values[:, 0:v_slots, i], in_=raw[:].indirect(offs_t[:, 0 : v_slots // 16]))
                 j0 = v_slots
                 for n in s_pieces:
                     nc.scalar.activation(

@@ -1,7 +1,6 @@
 from contextlib import ExitStack
 
 import concourse.mybir as mybir
-from concourse.masks import make_identity
 
 K, T, E, C, N = 1024, 2048, 4, 256, 128
 FLOPS = 2 * K * N * E * C
@@ -22,13 +21,13 @@ SLOTS = E * C
 PASSES = K // 512
 
 UNITS = (
-    (0, "plane", 0, ((2048, 512, 768),), 640, (384,)),
+    (0, "plane", 0, ((2048, 512, 1536),), 640, (384,)),
     (0, "plane", 1, ((2048, 512, 1536),), 640, (384,)),
     (0, "plane", 2, ((2048, 512, 1536),), 640, (384,)),
     (0, "plane", 3, ((2048, 512, 1536),), 640, (384,)),
-    (1, "pair", 0, ((1024, 512, 512), (1024, 256, 0)), 0, ()),
-    (1, "plane", 2, ((1024, 512, 512), (512, 256, 256), (512, 256, 256)), 320, (704,)),
-    (1, "plane", 3, ((768, 0, 768), (768, 0, 768), (512, 256, 256)), 320, (448, 256)),
+    (1, "pair", 0, ((1024, 512, 512), (1024, 256, 256)), 0, ()),
+    (1, "plane", 2, ((1024, 512, 512), (1024, 512, 512)), 320, (704,)),
+    (1, "plane", 3, ((768, 0, 768), (768, 0, 768), (512, 0, 512)), 320, (448, 256)),
 )
 QUANT_CUTS = ((1024,), (256, 256, 256, 256))
 SCATTER_CUTS = (1, 3)
@@ -43,20 +42,10 @@ def tile_routed_moe_kernel(tc, xT, w_words, w_scales, gate, offs, out):
 
         offs_t = lists.tile([P, SLOTS // 16], U16, name="offs_t")
 
-        gate_rows = keep.tile([P, P], F32, name="gate_rows")
-        nc.vector.memset(gate_rows[:], 0.0)
         w_scale_t = keep.tile([P, E * PASSES, N], U8, name="w_scale_t", align_bytes=64)
         nc.vector.memset(w_scale_t[:].rearrange("p i n -> p (i n)").bitcast(I32), 0)
         out_t = keep.tile([P, T], F32, name="out_t")
         nc.vector.memset(out_t[:], 0.0)
-
-        ident = keep.tile([P, P], F32, name="ident")
-        make_identity(nc, ident[:])
-        nc.sync.dma_start(out=gate_rows[0 : SLOTS // P, :], in_=gate[0, :].rearrange("(c n) -> c n", n=P))
-        cols_bank = psum.tile([P, P], F32, name="cols_bank")
-        nc.tensor.transpose(cols_bank[:], gate_rows[:], ident[:])
-        gate_cols = keep.tile([P, SLOTS // P], F32, name="gate_cols")
-        nc.scalar.copy(out=gate_cols[:], in_=cols_bank[:, 0 : SLOTS // P])
 
         planes = xT.rearrange("(g p t) n -> g p t n", p=P, t=4)
         scale_rows = w_scales.rearrange("e a (q r) n -> r q (e a) n", r=4)
@@ -84,11 +73,7 @@ def tile_routed_moe_kernel(tc, xT, w_words, w_scales, gate, offs, out):
         w_code_t = keep.tile([P, E * PASSES, N], I32, name="w_code_t", align_bytes=64)
         nc.sync.dma_start(out=w_code_t[:], in_=w_words.rearrange("e a p n r -> p (e a) (n r)").bitcast(I32))
         gate_t = keep.tile([P, SLOTS], F32, name="gate_t")
-        for h in range(2):
-            bank = psum.tile([P, SLOTS // 2], F32, name="gate_bank%d" % h)
-            for c in range(4):
-                nc.tensor.transpose(bank[:, c * P : (c + 1) * P], gate_cols[:, 4 * h + c : 4 * h + c + 1].to_broadcast([P, P]), ident[:])
-            nc.scalar.copy(out=gate_t[:, h * SLOTS // 2 : (h + 1) * SLOTS // 2], in_=bank[:])
+        nc.sync.dma_start(out=gate_t[:], in_=gate)
 
         grouped = [keep.tile([P, 4 * SLOTS], BF16, name="grouped%d" % g, align_bytes=64) for g in range(PASSES)]
         codes = [keep.tile([P, SLOTS], U32, name="codes%d" % g, align_bytes=64) for g in range(PASSES)]

@@ -21,13 +21,13 @@ SLOTS = E * C
 PASSES = K // 512
 
 UNITS = (
-    (0, "plane", 0, ((2048, 512, 1536),), 640, (384,)),
-    (0, "plane", 1, ((2048, 512, 1536),), 640, (384,)),
-    (0, "plane", 2, ((2048, 512, 1536),), 640, (384,)),
-    (0, "plane", 3, ((2048, 512, 1536),), 640, (384,)),
+    (0, "plane", 0, ((2048, 512, 1536),), 704, (320,)),
+    (0, "plane", 1, ((2048, 512, 1536),), 704, (320,)),
+    (0, "plane", 2, ((2048, 512, 1536),), 704, (320,)),
+    (0, "plane", 3, ((2048, 512, 1536),), 704, (320,)),
     (1, "pair", 0, ((1024, 512, 512), (1024, 256, 256)), 0, ()),
-    (1, "plane", 2, ((1024, 512, 512), (1024, 512, 512)), 320, (704,)),
-    (1, "plane", 3, ((768, 0, 768), (768, 0, 768), (512, 0, 512)), 320, (448, 256)),
+    (1, "plane", 2, ((1024, 512, 512), (512, 256, 256), (512, 256, 256)), 320, (704,)),
+    (1, "plane", 3, ((768, 0, 768), (768, 0, 768), (512, 128, 384)), 320, (448, 256)),
 )
 QUANT_CUTS = ((1024,), (256, 256, 256, 256))
 SCATTER_CUTS = (1, 3)

from contextlib import ExitStack

import concourse.mybir as mybir

K, T, E, C, N = 1024, 2048, 4, 256, 128
FLOPS = 2 * K * N * E * C

F32 = mybir.dt.float32
BF16 = mybir.dt.bfloat16
I32 = mybir.dt.int32
U32 = mybir.dt.uint32
U16 = mybir.dt.uint16
U8 = mybir.dt.uint8
FP8X4 = mybir.dt.float8_e4m3fn_x4
MULT = mybir.AluOpType.mult
ADD = mybir.AluOpType.add
COPY = mybir.ActivationFunctionType.Copy

P = 128
SLOTS = E * C
PASSES = K // 512

UNITS = (
    (0, "plane", 0, ((2048, 512, 1536),), 704, (320,)),
    (0, "plane", 1, ((2048, 512, 1536),), 704, (320,)),
    (0, "plane", 2, ((2048, 512, 1536),), 704, (320,)),
    (0, "plane", 3, ((2048, 512, 1536),), 704, (320,)),
    (1, "pair", 0, ((1024, 512, 512), (1024, 256, 256)), 0, ()),
    (1, "plane", 2, ((1024, 512, 512), (512, 256, 256), (512, 256, 256)), 320, (704,)),
    (1, "plane", 3, ((768, 0, 768), (768, 0, 768), (512, 128, 384)), 320, (448, 256)),
)
QUANT_CUTS = ((1024,), (256, 256, 256, 256))
SCATTER_CUTS = (1, 3)


def tile_routed_moe_kernel(tc, xT, w_words, w_scales, gate, offs, out):
    nc = tc.nc
    with ExitStack() as ctx:
        lists = ctx.enter_context(tc.tile_pool(name="lists", bufs=1))
        keep = ctx.enter_context(tc.tile_pool(name="keep", bufs=1))
        psum = ctx.enter_context(tc.psum_pool(name="psum", bufs=1))

        offs_t = lists.tile([P, SLOTS // 16], U16, name="offs_t")

        w_scale_t = keep.tile([P, E * PASSES, N], U8, name="w_scale_t", align_bytes=64)
        nc.vector.memset(w_scale_t[:].rearrange("p i n -> p (i n)").bitcast(I32), 0)
        out_t = keep.tile([P, T], F32, name="out_t")
        nc.vector.memset(out_t[:], 0.0)

        planes = xT.rearrange("(g p t) n -> g p t n", p=P, t=4)
        scale_rows = w_scales.rearrange("e a (q r) n -> r q (e a) n", r=4)

        raws = []
        first = True
        for g, kind, i, cuts, v_slots, s_pieces in UNITS:
            if kind == "pair":
                raw = keep.tile([P, 2, T], F32, name="rawpair%d_%d" % (g, i))
            else:
                raw = keep.tile([P, T], F32, name="rawplane%d_%d" % (g, i))
            raws.append(raw)
            c0 = 0
            for cols, s_cols, g_cols in cuts:
                if kind == "pair":
                    nc.sync.dma_start(out=raw[:, :, c0 : c0 + cols], in_=planes[g, :, 2 * i : 2 * i + 2, c0 : c0 + cols])
                else:
                    nc.sync.dma_start(out=raw[:, c0 : c0 + cols], in_=planes[g, :, i, c0 : c0 + cols])
                c0 += cols
                if first:
                    nc.sync.dma_start(offs_t[:], offs)
                    first = False
        for r in range(4):
            nc.sync.dma_start(out=w_scale_t[r:P:32, :, :].bitcast(I32), in_=scale_rows[r].bitcast(I32))
        w_code_t = keep.tile([P, E * PASSES, N], I32, name="w_code_t", align_bytes=64)
        nc.sync.dma_start(out=w_code_t[:], in_=w_words.rearrange("e a p n r -> p (e a) (n r)").bitcast(I32))
        gate_t = keep.tile([P, SLOTS], F32, name="gate_t")
        nc.sync.dma_start(out=gate_t[:], in_=gate)

        grouped = [keep.tile([P, 4 * SLOTS], BF16, name="grouped%d" % g, align_bytes=64) for g in range(PASSES)]
        codes = [keep.tile([P, SLOTS], U32, name="codes%d" % g, align_bytes=64) for g in range(PASSES)]
        scales = [keep.tile([P, SLOTS], U8, name="scales%d" % g, align_bytes=64) for g in range(PASSES)]
        acc = [psum.tile([P, C], F32, name="acc%d" % e) for e in range(E)]

        def cast(dst, src, cols, s_cols, g_cols):
            if s_cols > 0:
                nc.scalar.copy(out=dst[:, 0:s_cols], in_=src[:, 0:s_cols])
            if g_cols > 0:
                nc.gpsimd.tensor_scalar(
                    out=dst[:, s_cols : s_cols + g_cols],
                    in0=src[:, s_cols : s_cols + g_cols],
                    scalar1=1.0,
                    scalar2=0.0,
                    op0=MULT,
                    op1=ADD,
                )
            if s_cols + g_cols < cols:
                nc.vector.tensor_copy(out=dst[:, s_cols + g_cols : cols], in_=src[:, s_cols + g_cols : cols])

        done = [0] * PASSES
        for (g, kind, i, cuts, v_slots, s_pieces), raw in zip(UNITS, raws):
            if kind == "pair":
                pair = keep.tile([P, 2 * T], BF16, name="pair%d_%d" % (g, i))
                c0 = 0
                for cols, s_cols, g_cols in cuts:
                    cast(
                        pair[:, 2 * c0 : 2 * (c0 + cols)].rearrange("p (n e) -> p n e", e=2),
                        raw[:, :, c0 : c0 + cols].rearrange("p e n -> p n e"),
                        cols,
                        s_cols,
                        g_cols,
                    )
                    c0 += cols
                words = grouped[g][:].bitcast(U32).rearrange("p (j u) -> p j u", u=2)
                nc.vector.tensor_copy(out=words[:, :, i], in_=pair[:].bitcast(U32).indirect(offs_t[:]))
                done[g] += 2
            else:
                values = grouped[g][:].rearrange("p (j t) -> p j t", t=4)
                if s_pieces:
                    plane = keep.tile([P, T], BF16, name="plane%d_%d" % (g, i))
                    c0 = 0
                    for cols, s_cols, g_cols in cuts:
                        cast(plane[:, c0 : c0 + cols], raw[:, c0 : c0 + cols], cols, s_cols, g_cols)
                        c0 += cols
                nc.vector.tensor_copy(out=values[:, 0:v_slots, i], in_=raw[:].indirect(offs_t[:, 0 : v_slots // 16]))
                j0 = v_slots
                for n in s_pieces:
                    nc.scalar.activation(
                        out=values[:, j0 : j0 + n, i],
                        in_=plane[:].indirect(offs_t[:, j0 // 16 : (j0 + n) // 16]),
                        func=COPY,
                    )
                    j0 += n
                done[g] += 1
            if done[g] == 4:
                j0 = 0
                for n in QUANT_CUTS[g]:
                    nc.vector.quantize_mx(
                        out=codes[g][:, j0 : j0 + n].bitcast(FP8X4),
                        scales=scales[g][:, j0 : j0 + n],
                        in_=grouped[g][:, 4 * j0 : 4 * (j0 + n)],
                    )
                    j0 += n

        for g, e in ((0, 0), (1, 0), (0, 1), (0, 2), (0, 3), (1, 1), (1, 2), (1, 3)):
            js = slice(e * C, (e + 1) * C)
            nc.tensor.matmul_mx(
                out=acc[e][:],
                lhsT=w_code_t[:, PASSES * e + g, :].bitcast(FP8X4),
                lhsT_scale=w_scale_t[:, PASSES * e + g, :],
                rhs=codes[g][:, js].bitcast(FP8X4),
                rhs_scale=scales[g][:, js],
                start=(g == 0),
                stop=(g == PASSES - 1),
            )

        e0 = 0
        for s, experts in enumerate(SCATTER_CUTS):
            y = keep.tile([P, experts * C], F32, name="y%d" % s)
            for i in range(experts):
                nc.scalar.copy(out=y[:, i * C : (i + 1) * C], in_=acc[e0 + i][:])
            j0, j1 = e0 * C, (e0 + experts) * C
            nc.vector.tensor_tensor(
                out=out_t[:].indirect(offs_t[:, j0 // 16 : j1 // 16]),
                in0=y[:],
                in1=gate_t[:, j0:j1],
                op=MULT,
            )
            e0 += experts
        nc.sync.dma_start(out=out, in_=out_t[:])
